import numpy as np
import ml_dtypes


def mxq(x, axis, fmt="e4m3"):
    dtype, down = {"e4m3": (ml_dtypes.float8_e4m3fn, 7), "e5m2": (ml_dtypes.float8_e5m2, 14)}[fmt]
    v = np.moveaxis(np.asarray(x, np.float32).astype(ml_dtypes.bfloat16).astype(np.float64), axis, -1)
    blocks = v.reshape(v.shape[:-1] + (-1, 32))
    amax = np.abs(blocks).max(-1, keepdims=True)
    byte = np.maximum(np.where(amax > 0, np.frexp(amax)[1] - 1 + 127, 0) - down, 1)
    scale = np.exp2(byte - 127.0)
    codes = (blocks / scale).astype(np.float32).astype(dtype).astype(np.float64)
    return np.moveaxis((codes * scale).reshape(v.shape), -1, axis)


WIDE = False


def mx_kscale(k):
    if not WIDE:
        return np.ones(k)
    levels = np.array([10, -10, 5, -5, 0])
    if k % 512:
        return np.exp2(np.random.permutation(np.resize(levels, k // 32))).repeat(32)
    a = np.empty((k // 512, 16))
    for p in range(k // 512):
        a[p, :8] = np.random.permutation(np.resize(levels, 8))
        for g in range(8):
            far = levels[np.abs(levels - a[p, g]) >= 10]
            a[p, g + 8] = far[np.random.randint(len(far))]
    return np.exp2(a.ravel()).repeat(32)


def f64(x):
    return np.asarray(x).astype(np.float64)


def striped8(idx):
    return np.concatenate([v.reshape(-1, 16).T for v in idx]).astype(np.uint16)


def unstriped8(offs):
    return np.stack([offs[16 * g:16 * g + 16].T.reshape(-1) for g in range(8)]).astype(np.int64)


def split(x):
    m, e = np.frexp(f64(x))
    hi = np.ldexp(np.trunc(16.0 * m) / 16.0, e)
    return hi, f64(x) - hi


def gelu(v):
    return 0.5 * v * (1.0 + np.tanh(np.sqrt(2.0 / np.pi) * (v + 0.044715 * v**3)))


K, M, T, S = 1024, 128, 2048, 512


def setup_inputs():
    n = np.random.standard_normal
    s = mx_kscale(K)[:, None]
    return {
        "xT": (n((K, T)) * s).astype(np.float32),
        "w": (n((K, M)) / np.sqrt(K) / s).astype(np.float32),
        "wgt": np.repeat(np.random.uniform(0.5, 2.0, (8, S)), 16, axis=0).astype(np.float32),
        "b": (0.3 * n(128)).astype(np.float32),
        "offs": striped8(np.stack([np.random.permutation(T)[:S] for _ in range(8)])),
    }


def reference(xT, w, wgt, b, offs):
    idx = unstriped8(offs)
    group = np.arange(K) % 512 // 64
    xg = f64(wgt)[np.arange(K) // 4 % 128] * f64(xT)[np.arange(K)[:, None], idx[group]]
    xT_ = mxq(xg, 0, "e4m3")
    w_hi, w_lo = split(w)
    w_hi_, w_lo_ = mxq(w_hi, 0, "e4m3"), mxq(w_lo, 0, "e4m3")
    y = w_hi_.T @ xT_ + w_lo_.T @ xT_
    return gelu(y + f64(b)[:, None])

@@ -1,0 +1,139 @@
+from contextlib import ExitStack
+
+import concourse.mybir as mybir
+
+F32 = mybir.dt.float32
+BF16 = mybir.dt.bfloat16
+I32 = mybir.dt.int32
+U32 = mybir.dt.uint32
+U16 = mybir.dt.uint16
+U8 = mybir.dt.uint8
+FP8X4 = mybir.dt.float8_e4m3fn_x4
+MULT = mybir.AluOpType.mult
+SUB = mybir.AluOpType.subtract
+AND = mybir.AluOpType.bitwise_and
+GELU = mybir.ActivationFunctionType.Gelu_apprx_tanh
+
+K, M, T, S = 1024, 128, 2048, 512
+P = 128
+PACK = 4
+PASSES = K // (P * PACK)
+HALF = S // 2
+HEAD_BITS = -(1 << 20)
+
+FLOPS = 2 * 2 * K * M * S
+
+
+def tile_list_heads_hl_gelu_kernel(tc, xT, w, wgt, b, offs, out):
+    nc = tc.nc
+    with ExitStack() as ctx:
+        keep = ctx.enter_context(tc.tile_pool(name="keep", bufs=1))
+        psum = ctx.enter_context(tc.psum_pool(name="psum", bufs=1))
+
+        offsets = keep.tile([P, S // 16], U16, name="offsets")
+        nc.sync.dma_start(offsets[:], offs)
+        w_raw = keep.tile([P, PASSES, PACK, M], F32, name="w_raw")
+        nc.sync.dma_start(out=w_raw[:], in_=w.rearrange("(a p i) n -> p a i n", p=P, i=PACK))
+        weights = keep.tile([P, S], F32, name="weights")
+        nc.sync.dma_start(out=weights[:], in_=wgt)
+        bias = keep.tile([P, 1], F32, name="bias")
+        nc.scalar.dma_start(out=bias[:], in_=b.rearrange("(p o) -> p o", o=1))
+        planes_hbm = xT.rearrange("(a p i) t -> a i p t", p=P, i=PACK)
+        planes = {}
+        for a in range(PASSES):
+            for i in range(PACK):
+                planes[a, i] = keep.tile([P, T], F32, name=f"plane_{a}_{i}")
+                nc.sync.dma_start(out=planes[a, i][:], in_=planes_hbm[a, i])
+
+        zero = keep.tile([P, 1], F32, name="zero")
+        nc.vector.memset(zero[:], 0.0)
+        warm = keep.tile([P, 1], F32, name="warm")
+        nc.scalar.activation(warm[:], zero[:], GELU)
+
+        hi_bits = keep.tile([P, PASSES, PACK, M], I32, name="hi_bits")
+        nc.vector.tensor_scalar(hi_bits[:], w_raw[:].bitcast(I32), HEAD_BITS, None, AND)
+        hi_view = hi_bits[:].bitcast(F32).rearrange("p a i n -> p a n i")
+        w_grouped = {}
+        for name in ("hi", "lo"):
+            w_grouped[name] = keep.tile([P, PASSES, M, PACK], BF16, name=f"w_grouped_{name}", align_bytes=64)
+        nc.vector.tensor_tensor(w_grouped["lo"][:], w_raw[:].rearrange("p a i n -> p a n i"), hi_view, SUB)
+        nc.scalar.copy(w_grouped["hi"][:], hi_view)
+        w_codes, w_scales = {}, {}
+        for name in ("lo", "hi"):
+            w_codes[name] = keep.tile([P, PASSES * M], U32, name=f"w_codes_{name}", align_bytes=64)
+            w_scales[name] = keep.tile([P, PASSES * M], U8, name=f"w_scales_{name}", align_bytes=64)
+            nc.vector.quantize_mx(
+                out=w_codes[name][:].bitcast(FP8X4),
+                scales=w_scales[name][:],
+                in_=w_grouped[name][:].rearrange("p a n i -> p (a n i)"),
+            )
+
+        picked, grouped, codes, scales = {}, {}, {}, {}
+        for a in range(PASSES):
+            for h in range(2):
+                picked[a, h] = keep.tile([P, PACK, HALF], F32, name=f"picked_{a}_{h}")
+                grouped[a, h] = keep.tile([P, HALF, PACK], BF16, name=f"grouped_{a}_{h}", align_bytes=64)
+                codes[a, h] = keep.tile([P, HALF], U32, name=f"codes_{a}_{h}", align_bytes=64)
+                scales[a, h] = keep.tile([P, HALF], U8, name=f"scales_{a}_{h}", align_bytes=64)
+        acc = []
+        for h in range(2):
+            acc.append(psum.tile([M, HALF], F32, name=f"acc_{h}"))
+
+        def gather(a, i, h):
+            nc.vector.tensor_tensor(
+                picked[a, h][:, i, :],
+                planes[a, i][:].indirect(offsets[:, h * (HALF // 16) : (h + 1) * (HALF // 16)]),
+                weights[:, h * HALF : (h + 1) * HALF],
+                MULT,
+            )
+
+        def group(copy, a, h, i0, i1):
+            copy(grouped[a, h][:, :, i0:i1], picked[a, h][:, i0:i1, :].rearrange("p i j -> p j i"))
+
+        def quantize(a, h):
+            nc.vector.quantize_mx(
+                out=codes[a, h][:].bitcast(FP8X4),
+                scales=scales[a, h][:],
+                in_=grouped[a, h][:].rearrange("p j i -> p (j i)"),
+            )
+
+        def multiply(a, h):
+            for name in ("lo", "hi"):
+                cols = slice(a * M, (a + 1) * M)
+                nc.tensor.matmul_mx(
+                    out=acc[h][:],
+                    lhsT=w_codes[name][:, cols].bitcast(FP8X4),
+                    lhsT_scale=w_scales[name][:, cols],
+                    rhs=codes[a, h][:].bitcast(FP8X4),
+                    rhs_scale=scales[a, h][:],
+                    start=(a == 0 and name == "lo"),
+                    stop=(a == PASSES - 1 and name == "hi"),
+                )
+
+        for i in range(PACK):
+            for h in range(2):
+                gather(0, i, h)
+        for h in range(2):
+            group(nc.scalar.copy, 0, h, 0, PACK)
+        for h in range(2):
+            gather(1, 0, h)
+        for h in range(2):
+            quantize(0, h)
+            multiply(0, h)
+        for h in range(2):
+            gather(1, 1, h)
+        for h in range(2):
+            group(nc.scalar.copy, 1, h, 0, 2)
+        for h in range(2):
+            gather(1, 2, h)
+        gather(1, 3, 0)
+        group(nc.scalar.copy, 1, 0, 2, PACK)
+        gather(1, 3, 1)
+        group(nc.vector.tensor_copy, 1, 1, 2, PACK)
+        for h in range(2):
+            quantize(1, h)
+            multiply(1, h)
+        for h in range(2):
+            result = keep.tile([M, HALF], F32, name=f"result_{h}")
+            nc.scalar.activation(result[:], acc[h][:], GELU, bias=bias[:])
+            nc.sync.dma_start(out=out[:, h * HALF : (h + 1) * HALF], in_=result[:])

@@ -1,6 +1,7 @@
 from contextlib import ExitStack
 
 import concourse.mybir as mybir
+from concourse.masks import make_identity
 
 F32 = mybir.dt.float32
 BF16 = mybir.dt.bfloat16
@@ -18,10 +19,13 @@ K, M, T, S = 1024, 128, 2048, 512
 P = 128
 PACK = 4
 PASSES = K // (P * PACK)
+GROUP = 16
 HALF = S // 2
+CHUNKS = ((0, 128), (128, 256), (256, 384), (384, 512))
 HEAD_BITS = -(1 << 20)
 
 FLOPS = 2 * 2 * K * M * S
+BYTES = 4 * (K * T + K * M + P // GROUP * S + M + M * S) + 2 * P * (S // GROUP)
 
 
 def tile_list_heads_hl_gelu_kernel(tc, xT, w, wgt, b, offs, out):
@@ -30,14 +34,14 @@ def tile_list_heads_hl_gelu_kernel(tc, xT, w, wgt, b, offs, out):
         keep = ctx.enter_context(tc.tile_pool(name="keep", bufs=1))
         psum = ctx.enter_context(tc.psum_pool(name="psum", bufs=1))
 
-        offsets = keep.tile([P, S // 16], U16, name="offsets")
+        rows = keep.tile([P, S + M], F32, name="rows")
+        nc.vector.memset(rows[:], 0.0)
+        offsets = keep.tile([P, S // GROUP], U16, name="offsets")
         nc.sync.dma_start(offsets[:], offs)
         w_raw = keep.tile([P, PASSES, PACK, M], F32, name="w_raw")
         nc.sync.dma_start(out=w_raw[:], in_=w.rearrange("(a p i) n -> p a i n", p=P, i=PACK))
-        weights = keep.tile([P, S], F32, name="weights")
-        nc.sync.dma_start(out=weights[:], in_=wgt)
-        bias = keep.tile([P, 1], F32, name="bias")
-        nc.scalar.dma_start(out=bias[:], in_=b.rearrange("(p o) -> p o", o=1))
+        nc.sync.dma_start(out=rows[0 : P // GROUP, 0:S], in_=wgt.rearrange("(g r) j -> g r j", r=GROUP)[:, 0, :])
+        nc.sync.dma_start(out=rows[0:1, S : S + M], in_=b.rearrange("(o n) -> o n", o=1))
         planes_hbm = xT.rearrange("(a p i) t -> a i p t", p=P, i=PACK)
         planes = {}
         for a in range(PASSES):
@@ -45,10 +49,34 @@ def tile_list_heads_hl_gelu_kernel(tc, xT, w, wgt, b, offs, out):
                 planes[a, i] = keep.tile([P, T], F32, name=f"plane_{a}_{i}")
                 nc.sync.dma_start(out=planes[a, i][:], in_=planes_hbm[a, i])
 
+        identity = keep.tile([P, P], F32, name="identity")
+        make_identity(nc, identity[:])
+
         zero = keep.tile([P, 1], F32, name="zero")
         nc.vector.memset(zero[:], 0.0)
         warm = keep.tile([P, 1], F32, name="warm")
         nc.scalar.activation(warm[:], zero[:], GELU)
+
+        blocks = S // P
+        columns_ps = psum.tile([P, blocks, P], F32, name="columns_ps")
+        for c in range(blocks):
+            nc.tensor.transpose(columns_ps[:, c, :], rows[:, c * P : (c + 1) * P], identity[:])
+        bias_ps = psum.tile([P, P], F32, name="bias_ps")
+        nc.tensor.transpose(bias_ps[:], rows[:, S : S + M], identity[:])
+        repeated = keep.tile([P, blocks, P // GROUP, GROUP], F32, name="repeated")
+        nc.scalar.copy(
+            repeated[:],
+            columns_ps[:, :, 0 : P // GROUP].unsqueeze(3).to_broadcast([P, blocks, P // GROUP, GROUP]),
+        )
+        weights_ps = psum.tile([P, S], F32, name="weights_ps")
+        for c in range(blocks):
+            nc.tensor.transpose(
+                weights_ps[:, c * P : (c + 1) * P], repeated[:, c].rearrange("p g r -> p (g r)"), identity[:]
+            )
+        weights = keep.tile([P, S], F32, name="weights")
+        nc.scalar.copy(weights[:], weights_ps[:])
+        bias = keep.tile([P, 1], F32, name="bias")
+        nc.scalar.copy(bias[:], bias_ps[:, 0:1])
 
         hi_bits = keep.tile([P, PASSES, PACK, M], I32, name="hi_bits")
         nc.vector.tensor_scalar(hi_bits[:], w_raw[:].bitcast(I32), HEAD_BITS, None, AND)
@@ -68,72 +96,78 @@ def tile_list_heads_hl_gelu_kernel(tc, xT, w, wgt, b, offs, out):
                 in_=w_grouped[name][:].rearrange("p a n i -> p (a n i)"),
             )
 
-        picked, grouped, codes, scales = {}, {}, {}, {}
+        picked, grouped = {}, {}
+        codes = keep.tile([P, PASSES, S], U32, name="codes", align_bytes=64)
+        scales = keep.tile([P, PASSES, S], U8, name="scales", align_bytes=64)
         for a in range(PASSES):
-            for h in range(2):
-                picked[a, h] = keep.tile([P, PACK, HALF], F32, name=f"picked_{a}_{h}")
-                grouped[a, h] = keep.tile([P, HALF, PACK], BF16, name=f"grouped_{a}_{h}", align_bytes=64)
-                codes[a, h] = keep.tile([P, HALF], U32, name=f"codes_{a}_{h}", align_bytes=64)
-                scales[a, h] = keep.tile([P, HALF], U8, name=f"scales_{a}_{h}", align_bytes=64)
-        acc = []
-        for h in range(2):
-            acc.append(psum.tile([M, HALF], F32, name=f"acc_{h}"))
+            picked[a] = keep.tile([P, PACK, S], F32, name=f"picked_{a}")
+            grouped[a] = keep.tile([P, S, PACK], BF16, name=f"grouped_{a}", align_bytes=64)
+        acc = {}
+        for j0, j1 in CHUNKS:
+            acc[j0, j1] = psum.tile([M, j1 - j0], F32, name=f"acc_{j0}")
 
-        def gather(a, i, h):
+        def gather(a, i, j0, j1):
             nc.vector.tensor_tensor(
-                picked[a, h][:, i, :],
-                planes[a, i][:].indirect(offsets[:, h * (HALF // 16) : (h + 1) * (HALF // 16)]),
-                weights[:, h * HALF : (h + 1) * HALF],
+                picked[a][:, i, j0:j1],
+                planes[a, i][:].indirect(offsets[:, j0 // GROUP : j1 // GROUP]),
+                weights[:, j0:j1],
                 MULT,
             )
 
-        def group(copy, a, h, i0, i1):
-            copy(grouped[a, h][:, :, i0:i1], picked[a, h][:, i0:i1, :].rearrange("p i j -> p j i"))
+        def group(copy, a, i0, i1, j0, j1):
+            copy(grouped[a][:, j0:j1, i0:i1], picked[a][:, i0:i1, j0:j1].rearrange("p i j -> p j i"))
 
-        def quantize(a, h):
+        def quantize(a, j0, j1):
             nc.vector.quantize_mx(
-                out=codes[a, h][:].bitcast(FP8X4),
-                scales=scales[a, h][:],
-                in_=grouped[a, h][:].rearrange("p j i -> p (j i)"),
+                out=codes[:, a, j0:j1].bitcast(FP8X4),
+                scales=scales[:, a, j0:j1],
+                in_=grouped[a][:, j0:j1, :].rearrange("p j i -> p (j i)"),
             )
 
-        def multiply(a, h):
+        def multiply(a, j0, j1):
             for name in ("lo", "hi"):
                 cols = slice(a * M, (a + 1) * M)
                 nc.tensor.matmul_mx(
-                    out=acc[h][:],
+                    out=acc[j0, j1][:],
                     lhsT=w_codes[name][:, cols].bitcast(FP8X4),
                     lhsT_scale=w_scales[name][:, cols],
-                    rhs=codes[a, h][:].bitcast(FP8X4),
-                    rhs_scale=scales[a, h][:],
+                    rhs=codes[:, a, j0:j1].bitcast(FP8X4),
+                    rhs_scale=scales[:, a, j0:j1],
                     start=(a == 0 and name == "lo"),
                     stop=(a == PASSES - 1 and name == "hi"),
                 )
 
+        halves = ((0, HALF), (HALF, S))
         for i in range(PACK):
-            for h in range(2):
-                gather(0, i, h)
-        for h in range(2):
-            group(nc.scalar.copy, 0, h, 0, PACK)
-        for h in range(2):
-            gather(1, 0, h)
-        for h in range(2):
-            quantize(0, h)
-            multiply(0, h)
-        for h in range(2):
-            gather(1, 1, h)
-        for h in range(2):
-            group(nc.scalar.copy, 1, h, 0, 2)
-        for h in range(2):
-            gather(1, 2, h)
-        gather(1, 3, 0)
-        group(nc.scalar.copy, 1, 0, 2, PACK)
-        gather(1, 3, 1)
-        group(nc.vector.tensor_copy, 1, 1, 2, PACK)
-        for h in range(2):
-            quantize(1, h)
-            multiply(1, h)
+            for part in halves:
+                gather(0, i, *part)
+        for part in halves:
+            group(nc.scalar.copy, 0, 0, PACK, *part)
+        for part in halves:
+            gather(1, 0, *part)
+        quantize(0, 0, S)
+        for chunk in CHUNKS:
+            multiply(0, *chunk)
+        for part in halves:
+            gather(1, 1, *part)
+        for part in halves:
+            group(nc.scalar.copy, 1, 0, 2, *part)
+        for part in halves:
+            gather(1, 2, *part)
+        for j0, j1 in CHUNKS[:3]:
+            gather(1, 3, j0, j1)
+            group(nc.scalar.copy, 1, 2, PACK, j0, j1)
+        quantize(1, *CHUNKS[0])
+        multiply(1, *CHUNKS[0])
+        gather(1, 3, *CHUNKS[3])
+        quantize(1, *CHUNKS[1])
+        multiply(1, *CHUNKS[1])
+        group(nc.vector.tensor_copy, 1, 2, PACK, *CHUNKS[3])
+        for chunk in CHUNKS[2:]:
+            quantize(1, *chunk)
+            multiply(1, *chunk)
         for h in range(2):
             result = keep.tile([M, HALF], F32, name=f"result_{h}")
-            nc.scalar.activation(result[:], acc[h][:], GELU, bias=bias[:])
+            for j0, j1 in CHUNKS[2 * h : 2 * h + 2]:
+                nc.scalar.activation(result[:, j0 - h * HALF : j1 - h * HALF], acc[j0, j1][:], GELU, bias=bias[:])
             nc.sync.dma_start(out=out[:, h * HALF : (h + 1) * HALF], in_=result[:])

@@ -166,8 +166,7 @@ def tile_list_heads_hl_gelu_kernel(tc, xT, w, wgt, b, offs, out):
         for chunk in CHUNKS[2:]:
             quantize(1, *chunk)
             multiply(1, *chunk)
-        for h in range(2):
-            result = keep.tile([M, HALF], F32, name=f"result_{h}")
-            for j0, j1 in CHUNKS[2 * h : 2 * h + 2]:
-                nc.scalar.activation(result[:, j0 - h * HALF : j1 - h * HALF], acc[j0, j1][:], GELU, bias=bias[:])
-            nc.sync.dma_start(out=out[:, h * HALF : (h + 1) * HALF], in_=result[:])
+        for j0, j1 in CHUNKS:
+            result = keep.tile([M, j1 - j0], F32, name=f"result_{j0}")
+            nc.scalar.activation(result[:], acc[j0, j1][:], GELU, bias=bias[:])
+            nc.sync.dma_start(out=out[:, j0:j1], in_=result[:])

from contextlib import ExitStack

import concourse.mybir as mybir
from concourse.masks import make_identity

F32 = mybir.dt.float32
BF16 = mybir.dt.bfloat16
I32 = mybir.dt.int32
U32 = mybir.dt.uint32
U16 = mybir.dt.uint16
U8 = mybir.dt.uint8
FP8X4 = mybir.dt.float8_e4m3fn_x4
MULT = mybir.AluOpType.mult
SUB = mybir.AluOpType.subtract
AND = mybir.AluOpType.bitwise_and
GELU = mybir.ActivationFunctionType.Gelu_apprx_tanh

K, M, T, S = 1024, 128, 2048, 512
P = 128
PACK = 4
PASSES = K // (P * PACK)
GROUP = 16
HALF = S // 2
CHUNKS = ((0, 128), (128, 256), (256, 384), (384, 512))
HEAD_BITS = -(1 << 20)

FLOPS = 2 * 2 * K * M * S
BYTES = 4 * (K * T + K * M + P // GROUP * S + M + M * S) + 2 * P * (S // GROUP)


def tile_list_heads_hl_gelu_kernel(tc, xT, w, wgt, b, offs, out):
    nc = tc.nc
    with ExitStack() as ctx:
        keep = ctx.enter_context(tc.tile_pool(name="keep", bufs=1))
        psum = ctx.enter_context(tc.psum_pool(name="psum", bufs=1))

        rows = keep.tile([P, S + M], F32, name="rows")
        nc.vector.memset(rows[:], 0.0)
        offsets = keep.tile([P, S // GROUP], U16, name="offsets")
        nc.sync.dma_start(offsets[:], offs)
        w_raw = keep.tile([P, PASSES, PACK, M], F32, name="w_raw")
        nc.sync.dma_start(out=w_raw[:], in_=w.rearrange("(a p i) n -> p a i n", p=P, i=PACK))
        nc.sync.dma_start(out=rows[0 : P // GROUP, 0:S], in_=wgt.rearrange("(g r) j -> g r j", r=GROUP)[:, 0, :])
        nc.sync.dma_start(out=rows[0:1, S : S + M], in_=b.rearrange("(o n) -> o n", o=1))
        planes_hbm = xT.rearrange("(a p i) t -> a i p t", p=P, i=PACK)
        planes = {}
        for a in range(PASSES):
            for i in range(PACK):
                planes[a, i] = keep.tile([P, T], F32, name=f"plane_{a}_{i}")
                nc.sync.dma_start(out=planes[a, i][:], in_=planes_hbm[a, i])

        identity = keep.tile([P, P], F32, name="identity")
        make_identity(nc, identity[:])

        zero = keep.tile([P, 1], F32, name="zero")
        nc.vector.memset(zero[:], 0.0)
        warm = keep.tile([P, 1], F32, name="warm")
        nc.scalar.activation(warm[:], zero[:], GELU)

        blocks = S // P
        columns_ps = psum.tile([P, blocks, P], F32, name="columns_ps")
        for c in range(blocks):
            nc.tensor.transpose(columns_ps[:, c, :], rows[:, c * P : (c + 1) * P], identity[:])
        bias_ps = psum.tile([P, P], F32, name="bias_ps")
        nc.tensor.transpose(bias_ps[:], rows[:, S : S + M], identity[:])
        repeated = keep.tile([P, blocks, P // GROUP, GROUP], F32, name="repeated")
        nc.scalar.copy(
            repeated[:],
            columns_ps[:, :, 0 : P // GROUP].unsqueeze(3).to_broadcast([P, blocks, P // GROUP, GROUP]),
        )
        weights_ps = psum.tile([P, S], F32, name="weights_ps")
        for c in range(blocks):
            nc.tensor.transpose(
                weights_ps[:, c * P : (c + 1) * P], repeated[:, c].rearrange("p g r -> p (g r)"), identity[:]
            )
        weights = keep.tile([P, S], F32, name="weights")
        nc.scalar.copy(weights[:], weights_ps[:])
        bias = keep.tile([P, 1], F32, name="bias")
        nc.scalar.copy(bias[:], bias_ps[:, 0:1])

        hi_bits = keep.tile([P, PASSES, PACK, M], I32, name="hi_bits")
        nc.vector.tensor_scalar(hi_bits[:], w_raw[:].bitcast(I32), HEAD_BITS, None, AND)
        hi_view = hi_bits[:].bitcast(F32).rearrange("p a i n -> p a n i")
        w_grouped = {}
        for name in ("hi", "lo"):
            w_grouped[name] = keep.tile([P, PASSES, M, PACK], BF16, name=f"w_grouped_{name}", align_bytes=64)
        nc.vector.tensor_tensor(w_grouped["lo"][:], w_raw[:].rearrange("p a i n -> p a n i"), hi_view, SUB)
        nc.scalar.copy(w_grouped["hi"][:], hi_view)
        w_codes, w_scales = {}, {}
        for name in ("lo", "hi"):
            w_codes[name] = keep.tile([P, PASSES * M], U32, name=f"w_codes_{name}", align_bytes=64)
            w_scales[name] = keep.tile([P, PASSES * M], U8, name=f"w_scales_{name}", align_bytes=64)
            nc.vector.quantize_mx(
                out=w_codes[name][:].bitcast(FP8X4),
                scales=w_scales[name][:],
                in_=w_grouped[name][:].rearrange("p a n i -> p (a n i)"),
            )

        picked, grouped = {}, {}
        codes = keep.tile([P, PASSES, S], U32, name="codes", align_bytes=64)
        scales = keep.tile([P, PASSES, S], U8, name="scales", align_bytes=64)
        for a in range(PASSES):
            picked[a] = keep.tile([P, PACK, S], F32, name=f"picked_{a}")
            grouped[a] = keep.tile([P, S, PACK], BF16, name=f"grouped_{a}", align_bytes=64)
        acc = {}
        for j0, j1 in CHUNKS:
            acc[j0, j1] = psum.tile([M, j1 - j0], F32, name=f"acc_{j0}")

        def gather(a, i, j0, j1):
            nc.vector.tensor_tensor(
                picked[a][:, i, j0:j1],
                planes[a, i][:].indirect(offsets[:, j0 // GROUP : j1 // GROUP]),
                weights[:, j0:j1],
                MULT,
            )

        def group(copy, a, i0, i1, j0, j1):
            copy(grouped[a][:, j0:j1, i0:i1], picked[a][:, i0:i1, j0:j1].rearrange("p i j -> p j i"))

        def quantize(a, j0, j1):
            nc.vector.quantize_mx(
                out=codes[:, a, j0:j1].bitcast(FP8X4),
                scales=scales[:, a, j0:j1],
                in_=grouped[a][:, j0:j1, :].rearrange("p j i -> p (j i)"),
            )

        def multiply(a, j0, j1):
            for name in ("lo", "hi"):
                cols = slice(a * M, (a + 1) * M)
                nc.tensor.matmul_mx(
                    out=acc[j0, j1][:],
                    lhsT=w_codes[name][:, cols].bitcast(FP8X4),
                    lhsT_scale=w_scales[name][:, cols],
                    rhs=codes[:, a, j0:j1].bitcast(FP8X4),
                    rhs_scale=scales[:, a, j0:j1],
                    start=(a == 0 and name == "lo"),
                    stop=(a == PASSES - 1 and name == "hi"),
                )

        halves = ((0, HALF), (HALF, S))
        for i in range(PACK):
            for part in halves:
                gather(0, i, *part)
        for part in halves:
            group(nc.scalar.copy, 0, 0, PACK, *part)
        for part in halves:
            gather(1, 0, *part)
        quantize(0, 0, S)
        for chunk in CHUNKS:
            multiply(0, *chunk)
        for part in halves:
            gather(1, 1, *part)
        for part in halves:
            group(nc.scalar.copy, 1, 0, 2, *part)
        for part in halves:
            gather(1, 2, *part)
        for j0, j1 in CHUNKS[:3]:
            gather(1, 3, j0, j1)
            group(nc.scalar.copy, 1, 2, PACK, j0, j1)
        quantize(1, *CHUNKS[0])
        multiply(1, *CHUNKS[0])
        gather(1, 3, *CHUNKS[3])
        quantize(1, *CHUNKS[1])
        multiply(1, *CHUNKS[1])
        group(nc.vector.tensor_copy, 1, 2, PACK, *CHUNKS[3])
        for chunk in CHUNKS[2:]:
            quantize(1, *chunk)
            multiply(1, *chunk)
        for j0, j1 in CHUNKS:
            result = keep.tile([M, j1 - j0], F32, name=f"result_{j0}")
            nc.scalar.activation(result[:], acc[j0, j1][:], GELU, bias=bias[:])
            nc.sync.dma_start(out=out[:, j0:j1], in_=result[:])
